import numpy as np
import ml_dtypes


def mxq(x, axis, fmt="e4m3"):
    dtype, down = {"e4m3": (ml_dtypes.float8_e4m3fn, 7), "e5m2": (ml_dtypes.float8_e5m2, 14)}[fmt]
    v = np.moveaxis(np.asarray(x, np.float32).astype(ml_dtypes.bfloat16).astype(np.float64), axis, -1)
    blocks = v.reshape(v.shape[:-1] + (-1, 32))
    amax = np.abs(blocks).max(-1, keepdims=True)
    byte = np.maximum(np.where(amax > 0, np.frexp(amax)[1] - 1 + 127, 0) - down, 1)
    scale = np.exp2(byte - 127.0)
    codes = (blocks / scale).astype(np.float32).astype(dtype).astype(np.float64)
    return np.moveaxis((codes * scale).reshape(v.shape), -1, axis)


WIDE = False


def mx_kscale(k):
    if not WIDE:
        return np.ones(k)
    levels = np.array([10, -10, 5, -5, 0])
    if k % 512:
        return np.exp2(np.random.permutation(np.resize(levels, k // 32))).repeat(32)
    a = np.empty((k // 512, 16))
    for p in range(k // 512):
        a[p, :8] = np.random.permutation(np.resize(levels, 8))
        for g in range(8):
            far = levels[np.abs(levels - a[p, g]) >= 10]
            a[p, g + 8] = far[np.random.randint(len(far))]
    return np.exp2(a.ravel()).repeat(32)


def f64(x):
    return np.asarray(x).astype(np.float64)


def striped(idx):
    return np.tile(np.asarray(idx).reshape(-1, 16).T, (8, 1)).astype(np.uint16)


def unstriped(offs):
    return offs[:16].T.reshape(-1).astype(np.int64)


E2M1 = np.array([0.0, 0.5, 1.0, 1.5, 2.0, 3.0, 4.0, 6.0, -0.0, -0.5, -1.0, -1.5, -2.0, -3.0, -4.0, -6.0])


def pack_weight(w, fmt):
    k, n = w.shape
    w = f64(np.asarray(w, np.float32).astype(ml_dtypes.bfloat16)).reshape(k // 32, 32, n)
    amax = np.abs(w).max(1)
    if fmt == "e4m3":
        byte = np.frexp(amax)[1] - 1 + 127 - 7
    else:
        mant, ex = np.frexp(amax / 6.0)
        byte = np.where(mant > 0.5, ex, ex - 1) + 127
    byte = np.clip(np.where(amax > 0, byte, 1), 1, 254)
    scaled = (w * np.exp2(127.0 - byte)[:, None, :]).reshape(k, n).astype(np.float32)
    by_word = np.ascontiguousarray(scaled.reshape(k // 512, 128, 4, n).transpose(0, 1, 3, 2))
    if fmt == "e4m3":
        words = by_word.astype(ml_dtypes.float8_e4m3fn).view(np.uint8)
    else:
        c = by_word.astype(ml_dtypes.float4_e2m1fn).view(np.uint8) & 0xF
        words = (c[..., 0::2] | (c[..., 1::2] << 4)).reshape(k // 512, 128, 2 * n)
    return np.ascontiguousarray(words), np.ascontiguousarray(byte.astype(np.uint8).reshape(k // 512, 16, n))


def unpack_weight(words, scales, fmt):
    g, _, n = scales.shape
    words = np.ascontiguousarray(words).reshape(g, 128, n, -1)
    if fmt == "e4m3":
        vals = words.view(ml_dtypes.float8_e4m3fn).astype(np.float64)
    else:
        nib = np.empty((g, 128, n, 4), np.uint8)
        nib[..., 0::2] = words & 0xF
        nib[..., 1::2] = words >> 4
        vals = E2M1[nib]
    vals = vals * np.repeat(np.exp2(scales.astype(np.float64) - 127.0), 8, axis=1)[..., None]
    return vals.transpose(0, 1, 3, 2).reshape(g * 512, n)


def bf(x):
    return np.asarray(x, np.float32).astype(ml_dtypes.bfloat16)


def planes(Y):
    r, m = Y.shape
    b = f64(bf(Y)).reshape(r // 32, 32, m)
    amax = np.abs(b).max(1)
    byte = np.clip(np.where(amax > 0, np.frexp(amax)[1] - 1 + 127 - 7, 1), 1, 254)
    codes = (b * np.exp2(127.0 - byte)[:, None, :]).reshape(r, m).astype(np.float32).astype(ml_dtypes.float8_e4m3fn).view(np.uint8)
    words = codes.reshape(r // 512, 128, 4, m).transpose(0, 1, 3, 2)
    return np.ascontiguousarray(words), np.ascontiguousarray(byte.astype(np.uint8).reshape(r // 512, 16, m))


K, T, L, J, N = 512, 512, 512, 512, 512


def setup_inputs():
    n = np.random.standard_normal
    idx = np.random.randint(0, T, J)
    idx2 = np.random.randint(0, T, J)
    idx3 = np.random.randint(0, T, J)
    fk = mx_kscale(K)
    fl = mx_kscale(L)
    xtp = pack_weight(n((K, T)) / fk[:, None], "e4m3")
    skp = pack_weight(n((L, J)) / fl[:, None], "e2m1")
    wsp = pack_weight(n((L, N)) * 1 / np.sqrt(L) * fl[:, None], "e4m3")
    return {
        "xt_words": xtp[0],
        "xt_scales": xtp[1],
        "w": (n((K, N)) * 1 / np.sqrt(K) * fk[:, None]).astype(np.float32),
        "sk_words": skp[0],
        "sk_scales": skp[1],
        "ws_words": wsp[0],
        "ws_scales": wsp[1],
        "sa": (np.random.uniform(0.3, 0.8, (1, J))).astype(np.float32),
        "sb": (np.random.uniform(0.2, 0.5, (1, J))).astype(np.float32),
        "sd": (np.random.uniform(0.1, 0.4, (1, J))).astype(np.float32),
        "offs": striped(idx),
        "offs2": striped(idx2),
        "offs3": striped(idx3),
    }


def reference(xt_words, xt_scales, w, sk_words, sk_scales, ws_words, ws_scales, sa, sb, sd, offs, offs2, offs3):
    idx = unstriped(offs)
    idx2 = unstriped(offs2)
    idx3 = unstriped(offs3)
    xtu = unpack_weight(xt_words, xt_scales, "e4m3")
    sku = unpack_weight(sk_words, sk_scales, "e2m1")
    wsu = unpack_weight(ws_words, ws_scales, "e4m3")
    wq = mxq(f64(w), 0, "e4m3")
    z = wq.T @ xtu
    s = wsu.T @ sku
    b = f64(sa) * z[:, idx] + f64(sb) * z[:, idx2] + f64(sd) * z[:, idx3]
    y = b + s
    words, scales = planes(y)
    return y, words, scales

@@ -1,0 +1,212 @@
+from contextlib import ExitStack
+
+import concourse.mybir as mybir
+from concourse.masks import make_identity
+
+K, T, L, J, N = 512, 512, 512, 512, 512
+FLOPS = 2 * K * N * T + 2 * L * N * J
+
+F32 = mybir.dt.float32
+BF16 = mybir.dt.bfloat16
+I32 = mybir.dt.int32
+U32 = mybir.dt.uint32
+U16 = mybir.dt.uint16
+U8 = mybir.dt.uint8
+FP8X4 = mybir.dt.float8_e4m3fn_x4
+FP4X4 = mybir.dt.float4_e2m1fn_x4
+MULT = mybir.AluOpType.mult
+ADD = mybir.AluOpType.add
+
+P = 128
+PACK = 4
+BLOCK = 128
+BLOCKS = J // BLOCK
+HALF = J // 2
+LIST_COLS = 16
+W_PIECES = ((0, 256), (256, 384), (384, 512))
+
+
+def load_scale_rows(queue, plane, rows):
+    for q in range(4):
+        queue.dma_start(out=plane[32 * q : 32 * q + 4, :].bitcast(I32), in_=rows[0, 4 * q : 4 * q + 4, :].bitcast(I32))
+
+
+def tile_list_three_point_blend_pl_kernel(
+    tc, xt_words, xt_scales, w, sk_words, sk_scales, ws_words, ws_scales, sa, sb, sd, offs, offs2, offs3, out_0, out_1, out_2
+):
+    nc = tc.nc
+    with ExitStack() as ctx:
+        sbuf = ctx.enter_context(tc.tile_pool(name="sbuf", bufs=1))
+        psum = ctx.enter_context(tc.psum_pool(name="psum", bufs=1))
+
+        def bank(b, name):
+            return psum.tile([P, 512], F32, name=name, tag="bank%d" % b)
+
+        lists = [sbuf.tile([P, J // LIST_COLS], U16, name="list%d" % i) for i in range(3)]
+        xt_plane = sbuf.tile([P, T], U8, align_bytes=64)
+        sk_plane = sbuf.tile([P, J], U8, align_bytes=64)
+        ws_plane = sbuf.tile([P, N], U8, align_bytes=64)
+        for plane in (xt_plane, sk_plane, ws_plane):
+            nc.vector.memset(plane[:].bitcast(U32), 0)
+        identity = sbuf.tile([P, P], F32)
+        make_identity(nc, identity[:])
+
+        share_cols = [sbuf.tile([P, PACK], F32, name="share_col%d" % i) for i in range(3)]
+        for col, share in zip(share_cols, (sa, sb, sd)):
+            nc.sync.dma_start(out=col[:], in_=share.rearrange("o (q m) -> (o q) m", m=PACK))
+
+        w_rows = w.rearrange("(p r) n -> p r n", r=PACK)
+        w_raw = [sbuf.tile([P, PACK, n1 - n0], F32, name="w_raw%d" % n0) for n0, n1 in W_PIECES]
+        for raw, (n0, n1) in zip(w_raw, W_PIECES):
+            nc.sync.dma_start(out=raw[:], in_=w_rows[:, :, n0:n1])
+        xt_codes = sbuf.tile([P, T], I32, align_bytes=64)
+        nc.sync.dma_start(out=xt_codes[:], in_=xt_words[0].rearrange("p c r -> p (c r)").bitcast(I32))
+        load_scale_rows(nc.sync, xt_plane, xt_scales)
+        for tile, src in zip(lists, (offs, offs2, offs3)):
+            nc.sync.dma_start(tile[:], src)
+        ws_codes = sbuf.tile([P, N], I32, align_bytes=64)
+        nc.sync.dma_start(out=ws_codes[:], in_=ws_words[0].rearrange("p c r -> p (c r)").bitcast(I32))
+        sk_codes = sbuf.tile([P, 2 * J], U8, align_bytes=64)
+        nc.sync.dma_start(out=sk_codes[:].bitcast(I32), in_=sk_words[0].bitcast(I32))
+        load_scale_rows(nc.sync, ws_plane, ws_scales)
+        load_scale_rows(nc.sync, sk_plane, sk_scales)
+
+        shares = []
+        for i in range(3):
+            spread = bank(4 + i, "spread%d" % i)
+            for m in range(PACK):
+                nc.tensor.transpose(spread[:, m * P : (m + 1) * P], share_cols[i][:, m : m + 1].to_broadcast([P, P]), identity[:])
+            share = sbuf.tile([P, J], F32, name="share%d" % i)
+            nc.scalar.copy(out=share[:].rearrange("p (q m) -> p q m", m=PACK), in_=spread[:].rearrange("p (m q) -> p q m", m=PACK))
+            shares.append(share)
+
+        w_bf = sbuf.tile([P, PACK, P, PACK], BF16, align_bytes=64)
+        for raw, (n0, n1) in zip(w_raw, W_PIECES):
+            nc.vector.tensor_copy(
+                out=w_bf[:, :, n0 // PACK : n1 // PACK, :].rearrange("p t m r -> p m t r"),
+                in_=raw[:].rearrange("p r (m t) -> p m t r", t=PACK),
+            )
+        w_codes = sbuf.tile([P, N], U32, align_bytes=64)
+        w_plane = sbuf.tile([P, N], U8, align_bytes=64)
+        for t0, t1 in ((0, 1), (1, 2), (2, 4)):
+            nc.vector.quantize_mx(
+                out=w_codes[:, t0 * P : t1 * P].bitcast(FP8X4),
+                scales=w_plane[:, t0 * P : t1 * P],
+                in_=w_bf[:, t0:t1].rearrange("p t m r -> p (t m r)"),
+            )
+
+        def z_columns(acc, t, c0, c1):
+            nc.tensor.matmul_mx(
+                out=acc[:, 0 : c1 - c0],
+                lhsT=w_codes[:, t * P : (t + 1) * P].bitcast(FP8X4),
+                lhsT_scale=w_plane[:, t * P : (t + 1) * P],
+                rhs=xt_codes[:, c0:c1].bitcast(FP8X4),
+                rhs_scale=xt_plane[:, c0:c1],
+                start=True,
+                stop=True,
+            )
+
+        z = [sbuf.tile([P, T], F32, name="z%d" % t) for t in range(PACK)]
+        acc = bank(0, "z_acc0_low")
+        z_columns(acc, 0, 0, T // 2)
+        nc.scalar.copy(out=z[0][:, 0 : T // 2], in_=acc[:, 0 : T // 2])
+        acc = bank(7, "z_acc0_high")
+        z_columns(acc, 0, T // 2, T)
+        nc.vector.tensor_copy(out=z[0][:, T // 2 : T], in_=acc[:, 0 : T // 2])
+        for t in range(1, PACK):
+            acc = bank(t, "z_acc%d" % t)
+            z_columns(acc, t, 0, T)
+            nc.scalar.copy(out=z[t][:], in_=acc[:])
+
+        skip = []
+        for b in range(BLOCKS):
+            acc = bank(4 + b, "s_acc%d" % b)
+            nc.tensor.matmul_mx(
+                out=acc[:],
+                lhsT=sk_codes[:, 2 * b * BLOCK : 2 * (b + 1) * BLOCK].bitcast(FP4X4),
+                lhsT_scale=sk_plane[:, b * BLOCK : (b + 1) * BLOCK],
+                rhs=ws_codes[:].bitcast(FP8X4),
+                rhs_scale=ws_plane[:],
+                start=True,
+                stop=True,
+            )
+            s_b = sbuf.tile([P, PACK, P], F32, name="skip%d" % b)
+            nc.scalar.copy(out=s_b[:], in_=acc[:].rearrange("j (p t) -> j t p", t=PACK))
+            skip.append(s_b)
+
+        y_codes = sbuf.tile([P, J], U32, align_bytes=64)
+        y_plane = sbuf.tile([P, J], U8, align_bytes=64)
+        out_rows = out_0.rearrange("(p t) j -> p t j", t=PACK)
+        out_words = out_1[0].rearrange("p c r -> p (c r)").bitcast(I32)
+
+        def gather(out, i, t, j0, j1):
+            offsets = lists[i][:, j0 // LIST_COLS : j1 // LIST_COLS]
+            nc.vector.tensor_tensor(out, z[t][:].indirect(offsets), shares[i][:, j0:j1], MULT)
+
+        def turn(out, src, start, stop):
+            nc.tensor.matmul(out, lhsT=src, rhs=identity[:], is_transpose=True, start=start, stop=stop)
+
+        def summed_on_tensor(half, terms, turned_banks, sum_banks):
+            blocks = (2 * half, 2 * half + 1)
+            turned = [bank(turned_banks[u], "turned%d" % blocks[u]) for u in range(2)]
+            for t in range(PACK):
+                for i in range(terms):
+                    picked = sbuf.tile([P, HALF], F32, name="picked%d_%d_%d" % (half, t, i))
+                    gather(picked[:], i, t, half * HALF, (half + 1) * HALF)
+                    for u in range(2):
+                        turn(
+                            turned[u][:, t * P : (t + 1) * P],
+                            picked[:, u * BLOCK : (u + 1) * BLOCK],
+                            t == 0 and i == 0,
+                            t == PACK - 1 and i == terms - 1,
+                        )
+            sums = []
+            for u in range(2):
+                total = bank(sum_banks[u], "sum%d" % blocks[u])
+                for t in range(PACK):
+                    turn(total[:, t * BLOCK : (t + 1) * BLOCK], skip[blocks[u]][:, t, :], t == 0, False)
+                sums.append(total)
+            for u in range(2):
+                blend = sbuf.tile([P, PACK * P], F32, name="blend%d" % blocks[u])
+                nc.scalar.copy(out=blend[:], in_=turned[u][:])
+                for t in range(PACK):
+                    turn(sums[u][:, t * BLOCK : (t + 1) * BLOCK], blend[:, t * P : (t + 1) * P], False, t == PACK - 1)
+            return sums
+
+        def quantize(y_bf, j0, j1):
+            nc.vector.quantize_mx(
+                out=y_codes[:, j0:j1].bitcast(FP8X4), scales=y_plane[:, j0:j1], in_=y_bf[:].rearrange("p j t -> p (j t)")
+            )
+
+        sums = summed_on_tensor(0, 3, (0, 1), (2, 3))
+        low_bf = sbuf.tile([P, HALF, PACK], BF16, align_bytes=64)
+        for b in range(2):
+            y_b = sbuf.tile([P, PACK, BLOCK], F32, name="y%d" % b)
+            total = sums[b][:].rearrange("p (t j) -> p t j", t=PACK)
+            nc.scalar.copy(out=y_b[:], in_=total)
+            nc.sync.dma_start(out=out_rows[:, :, b * BLOCK : (b + 1) * BLOCK], in_=y_b[:])
+            nc.scalar.copy(out=low_bf[:, b * BLOCK : (b + 1) * BLOCK, :], in_=total.rearrange("p t j -> p j t"))
+
+        sums = summed_on_tensor(1, 2, (4, 5), (6, 7))
+        quantize(low_bf, 0, HALF)
+        nc.sync.dma_start(out=out_words[:, 0:HALF], in_=y_codes[:, 0:HALF].bitcast(I32))
+
+        for b in range(2, BLOCKS):
+            third = sbuf.tile([P, PACK, BLOCK], F32, name="third%d" % b)
+            for t in range(PACK):
+                gather(third[:, t, :], 2, t, b * BLOCK, (b + 1) * BLOCK)
+            total = sums[b - 2][:].rearrange("p (t j) -> p t j", t=PACK)
+            y_b = sbuf.tile([P, PACK, BLOCK], F32, name="y%d" % b)
+            y_bf = sbuf.tile([P, BLOCK, PACK], BF16, name="y_bf%d" % b, align_bytes=64)
+            if b < BLOCKS - 1:
+                nc.vector.tensor_tensor(y_b[:], total, third[:], ADD)
+                nc.scalar.copy(out=y_bf[:], in_=y_b[:].rearrange("p t j -> p j t"))
+            else:
+                nc.vector.tensor_tensor(y_bf[:], total.rearrange("p t j -> p j t"), third[:].rearrange("p t j -> p j t"), ADD)
+                nc.vector.tensor_tensor(y_b[:], total, third[:], ADD)
+            nc.sync.dma_start(out=out_rows[:, :, b * BLOCK : (b + 1) * BLOCK], in_=y_b[:])
+            quantize(y_bf, b * BLOCK, (b + 1) * BLOCK)
+        nc.scalar.dma_start(out=out_words[:, HALF:J], in_=y_codes[:, HALF:J].bitcast(I32))
+        for q in range(4):
+            queue = nc.sync if q % 2 == 0 else nc.scalar
+            queue.dma_start(out=out_2[0, 4 * q : 4 * q + 4, :].bitcast(I32), in_=y_plane[32 * q : 32 * q + 4, :].bitcast(I32))

@@ -23,6 +23,7 @@ BLOCK = 128
 BLOCKS = J // BLOCK
 HALF = J // 2
 LIST_COLS = 16
+RING = 8
 W_PIECES = ((0, 256), (256, 384), (384, 512))
 
 
@@ -39,8 +40,8 @@ def tile_list_three_point_blend_pl_kernel(
         sbuf = ctx.enter_context(tc.tile_pool(name="sbuf", bufs=1))
         psum = ctx.enter_context(tc.psum_pool(name="psum", bufs=1))
 
-        def bank(b, name):
-            return psum.tile([P, 512], F32, name=name, tag="bank%d" % b)
+        banks = [psum.tile([P, 512], F32, name="bank%d" % b) for b in range(8)]
+        ring = sbuf.tile([P, RING * HALF], F32)
 
         lists = [sbuf.tile([P, J // LIST_COLS], U16, name="list%d" % i) for i in range(3)]
         xt_plane = sbuf.tile([P, T], U8, align_bytes=64)
@@ -50,15 +51,18 @@ def tile_list_three_point_blend_pl_kernel(
             nc.vector.memset(plane[:].bitcast(U32), 0)
         identity = sbuf.tile([P, P], F32)
         make_identity(nc, identity[:])
-
-        share_cols = [sbuf.tile([P, PACK], F32, name="share_col%d" % i) for i in range(3)]
-        for col, share in zip(share_cols, (sa, sb, sd)):
-            nc.sync.dma_start(out=col[:], in_=share.rearrange("o (q m) -> (o q) m", m=PACK))
+        load_scale_rows(nc.gpsimd, ws_plane, ws_scales)
 
         w_rows = w.rearrange("(p r) n -> p r n", r=PACK)
         w_raw = [sbuf.tile([P, PACK, n1 - n0], F32, name="w_raw%d" % n0) for n0, n1 in W_PIECES]
+        share_cols = [sbuf.tile([P, PACK], F32, name="share_col%d" % i) for i in range(3)]
+        share_rows = [share.rearrange("o (q m) -> (o q) m", m=PACK) for share in (sa, sb, sd)]
+        nc.sync.dma_start(out=share_cols[0][:], in_=share_rows[0])
         for raw, (n0, n1) in zip(w_raw, W_PIECES):
             nc.sync.dma_start(out=raw[:], in_=w_rows[:, :, n0:n1])
+            if n0 == 0:
+                for i in (1, 2):
+                    nc.sync.dma_start(out=share_cols[i][:], in_=share_rows[i])
         xt_codes = sbuf.tile([P, T], I32, align_bytes=64)
         nc.sync.dma_start(out=xt_codes[:], in_=xt_words[0].rearrange("p c r -> p (c r)").bitcast(I32))
         load_scale_rows(nc.sync, xt_plane, xt_scales)
@@ -68,12 +72,11 @@ def tile_list_three_point_blend_pl_kernel(
         nc.sync.dma_start(out=ws_codes[:], in_=ws_words[0].rearrange("p c r -> p (c r)").bitcast(I32))
         sk_codes = sbuf.tile([P, 2 * J], U8, align_bytes=64)
         nc.sync.dma_start(out=sk_codes[:].bitcast(I32), in_=sk_words[0].bitcast(I32))
-        load_scale_rows(nc.sync, ws_plane, ws_scales)
         load_scale_rows(nc.sync, sk_plane, sk_scales)
 
         shares = []
         for i in range(3):
-            spread = bank(4 + i, "spread%d" % i)
+            spread = banks[4 + i]
             for m in range(PACK):
                 nc.tensor.transpose(spread[:, m * P : (m + 1) * P], share_cols[i][:, m : m + 1].to_broadcast([P, P]), identity[:])
             share = sbuf.tile([P, J], F32, name="share%d" % i)
@@ -107,20 +110,20 @@ def tile_list_three_point_blend_pl_kernel(
             )
 
         z = [sbuf.tile([P, T], F32, name="z%d" % t) for t in range(PACK)]
-        acc = bank(0, "z_acc0_low")
+        acc = banks[0]
         z_columns(acc, 0, 0, T // 2)
         nc.scalar.copy(out=z[0][:, 0 : T // 2], in_=acc[:, 0 : T // 2])
-        acc = bank(7, "z_acc0_high")
+        acc = banks[1]
         z_columns(acc, 0, T // 2, T)
         nc.vector.tensor_copy(out=z[0][:, T // 2 : T], in_=acc[:, 0 : T // 2])
         for t in range(1, PACK):
-            acc = bank(t, "z_acc%d" % t)
+            acc = banks[(2, 3, 7)[t - 1]]
             z_columns(acc, t, 0, T)
             nc.scalar.copy(out=z[t][:], in_=acc[:])
 
         skip = []
         for b in range(BLOCKS):
-            acc = bank(4 + b, "s_acc%d" % b)
+            acc = banks[(4, 5, 6, 0)[b]]
             nc.tensor.matmul_mx(
                 out=acc[:],
                 lhsT=sk_codes[:, 2 * b * BLOCK : 2 * (b + 1) * BLOCK].bitcast(FP4X4),
@@ -146,13 +149,14 @@ def tile_list_three_point_blend_pl_kernel(
         def turn(out, src, start, stop):
             nc.tensor.matmul(out, lhsT=src, rhs=identity[:], is_transpose=True, start=start, stop=stop)
 
-        def summed_on_tensor(half, terms, turned_banks, sum_banks):
+        def summed_on_tensor(half, terms, first, turned_banks, sum_banks):
             blocks = (2 * half, 2 * half + 1)
-            turned = [bank(turned_banks[u], "turned%d" % blocks[u]) for u in range(2)]
+            turned = [banks[turned_banks[u]] for u in range(2)]
             for t in range(PACK):
                 for i in range(terms):
-                    picked = sbuf.tile([P, HALF], F32, name="picked%d_%d_%d" % (half, t, i))
-                    gather(picked[:], i, t, half * HALF, (half + 1) * HALF)
+                    slot = (first + t * terms + i) % RING
+                    picked = ring[:, slot * HALF : (slot + 1) * HALF]
+                    gather(picked, i, t, half * HALF, (half + 1) * HALF)
                     for u in range(2):
                         turn(
                             turned[u][:, t * P : (t + 1) * P],
@@ -162,7 +166,7 @@ def tile_list_three_point_blend_pl_kernel(
                         )
             sums = []
             for u in range(2):
-                total = bank(sum_banks[u], "sum%d" % blocks[u])
+                total = banks[sum_banks[u]]
                 for t in range(PACK):
                     turn(total[:, t * BLOCK : (t + 1) * BLOCK], skip[blocks[u]][:, t, :], t == 0, False)
                 sums.append(total)
@@ -173,12 +177,15 @@ def tile_list_three_point_blend_pl_kernel(
                     turn(sums[u][:, t * BLOCK : (t + 1) * BLOCK], blend[:, t * P : (t + 1) * P], False, t == PACK - 1)
             return sums
 
+        def woven(rows):
+            return rows.rearrange("p t (c i) -> p c t i", i=4)
+
         def quantize(y_bf, j0, j1):
             nc.vector.quantize_mx(
                 out=y_codes[:, j0:j1].bitcast(FP8X4), scales=y_plane[:, j0:j1], in_=y_bf[:].rearrange("p j t -> p (j t)")
             )
 
-        sums = summed_on_tensor(0, 3, (0, 1), (2, 3))
+        sums = summed_on_tensor(0, 3, 0, (4, 5), (1, 2))
         low_bf = sbuf.tile([P, HALF, PACK], BF16, align_bytes=64)
         for b in range(2):
             y_b = sbuf.tile([P, PACK, BLOCK], F32, name="y%d" % b)
@@ -187,25 +194,27 @@ def tile_list_three_point_blend_pl_kernel(
             nc.sync.dma_start(out=out_rows[:, :, b * BLOCK : (b + 1) * BLOCK], in_=y_b[:])
             nc.scalar.copy(out=low_bf[:, b * BLOCK : (b + 1) * BLOCK, :], in_=total.rearrange("p t j -> p j t"))
 
-        sums = summed_on_tensor(1, 2, (4, 5), (6, 7))
+        sums = summed_on_tensor(1, 2, 12, (4, 5), (3, 7))
         quantize(low_bf, 0, HALF)
         nc.sync.dma_start(out=out_words[:, 0:HALF], in_=y_codes[:, 0:HALF].bitcast(I32))
 
+        high_bf = sbuf.tile([P, HALF, PACK], BF16, align_bytes=64)
+        third = ring[:, 4 * HALF : 8 * HALF].rearrange("p (t j) -> p t j", t=PACK)
+        for t in range(PACK):
+            gather(third[:, t, :], 2, t, HALF, J)
         for b in range(2, BLOCKS):
-            third = sbuf.tile([P, PACK, BLOCK], F32, name="third%d" % b)
-            for t in range(PACK):
-                gather(third[:, t, :], 2, t, b * BLOCK, (b + 1) * BLOCK)
+            last = third[:, :, (b - 2) * BLOCK : (b - 1) * BLOCK]
             total = sums[b - 2][:].rearrange("p (t j) -> p t j", t=PACK)
             y_b = sbuf.tile([P, PACK, BLOCK], F32, name="y%d" % b)
-            y_bf = sbuf.tile([P, BLOCK, PACK], BF16, name="y_bf%d" % b, align_bytes=64)
+            y_bf = high_bf[:, (b - 2) * BLOCK : (b - 1) * BLOCK, :].rearrange("p (c i) t -> p c t i", i=4)
             if b < BLOCKS - 1:
-                nc.vector.tensor_tensor(y_b[:], total, third[:], ADD)
-                nc.scalar.copy(out=y_bf[:], in_=y_b[:].rearrange("p t j -> p j t"))
+                nc.vector.tensor_tensor(y_b[:], total, last, ADD)
+                nc.scalar.copy(out=y_bf, in_=woven(y_b[:]))
             else:
-                nc.vector.tensor_tensor(y_bf[:], total.rearrange("p t j -> p j t"), third[:].rearrange("p t j -> p j t"), ADD)
-                nc.vector.tensor_tensor(y_b[:], total, third[:], ADD)
+                nc.vector.tensor_tensor(y_bf, woven(total), woven(last), ADD)
+                nc.vector.tensor_tensor(y_b[:], total, last, ADD)
             nc.sync.dma_start(out=out_rows[:, :, b * BLOCK : (b + 1) * BLOCK], in_=y_b[:])
-            quantize(y_bf, b * BLOCK, (b + 1) * BLOCK)
+        quantize(high_bf, HALF, J)
         nc.scalar.dma_start(out=out_words[:, HALF:J], in_=y_codes[:, HALF:J].bitcast(I32))
         for q in range(4):
             queue = nc.sync if q % 2 == 0 else nc.scalar

@@ -24,7 +24,6 @@ BLOCKS = J // BLOCK
 HALF = J // 2
 LIST_COLS = 16
 RING = 8
-W_PIECES = ((0, 256), (256, 384), (384, 512))
 
 
 def load_scale_rows(queue, plane, rows):
@@ -54,15 +53,14 @@ def tile_list_three_point_blend_pl_kernel(
         load_scale_rows(nc.gpsimd, ws_plane, ws_scales)
 
         w_rows = w.rearrange("(p r) n -> p r n", r=PACK)
-        w_raw = [sbuf.tile([P, PACK, n1 - n0], F32, name="w_raw%d" % n0) for n0, n1 in W_PIECES]
+        w_raw = [sbuf.tile([P, 2, N], F32, name="w_raw%d" % h) for h in range(2)]
         share_cols = [sbuf.tile([P, PACK], F32, name="share_col%d" % i) for i in range(3)]
         share_rows = [share.rearrange("o (q m) -> (o q) m", m=PACK) for share in (sa, sb, sd)]
         nc.sync.dma_start(out=share_cols[0][:], in_=share_rows[0])
-        for raw, (n0, n1) in zip(w_raw, W_PIECES):
-            nc.sync.dma_start(out=raw[:], in_=w_rows[:, :, n0:n1])
-            if n0 == 0:
-                for i in (1, 2):
-                    nc.sync.dma_start(out=share_cols[i][:], in_=share_rows[i])
+        nc.sync.dma_start(out=w_raw[0][:], in_=w_rows[:, 0:2, :])
+        nc.sync.dma_start(out=share_cols[1][:], in_=share_rows[1])
+        nc.sync.dma_start(out=share_cols[2][:], in_=share_rows[2])
+        nc.sync.dma_start(out=w_raw[1][:], in_=w_rows[:, 2:4, :])
         xt_codes = sbuf.tile([P, T], I32, align_bytes=64)
         nc.sync.dma_start(out=xt_codes[:], in_=xt_words[0].rearrange("p c r -> p (c r)").bitcast(I32))
         load_scale_rows(nc.sync, xt_plane, xt_scales)
@@ -84,19 +82,29 @@ def tile_list_three_point_blend_pl_kernel(
             shares.append(share)
 
         w_bf = sbuf.tile([P, PACK, P, PACK], BF16, align_bytes=64)
-        for raw, (n0, n1) in zip(w_raw, W_PIECES):
-            nc.vector.tensor_copy(
-                out=w_bf[:, :, n0 // PACK : n1 // PACK, :].rearrange("p t m r -> p m t r"),
-                in_=raw[:].rearrange("p r (m t) -> p m t r", t=PACK),
-            )
         w_codes = sbuf.tile([P, N], U32, align_bytes=64)
         w_plane = sbuf.tile([P, N], U8, align_bytes=64)
-        for t0, t1 in ((0, 1), (1, 2), (2, 4)):
+
+        def round_w(h, t0, t1):
+            nc.vector.tensor_copy(
+                out=w_bf[:, t0:t1, :, 2 * h : 2 * h + 2].rearrange("p t m r -> p m t r"),
+                in_=w_raw[h][:].rearrange("p r (m t) -> p m t r", t=PACK)[:, :, t0:t1, :],
+            )
+
+        def quantize_w(t0, t1):
             nc.vector.quantize_mx(
                 out=w_codes[:, t0 * P : t1 * P].bitcast(FP8X4),
                 scales=w_plane[:, t0 * P : t1 * P],
                 in_=w_bf[:, t0:t1].rearrange("p t m r -> p (t m r)"),
             )
+
+        round_w(0, 0, PACK)
+        round_w(1, 0, 1)
+        round_w(1, 1, 2)
+        quantize_w(0, 1)
+        round_w(1, 2, PACK)
+        quantize_w(1, 2)
+        quantize_w(2, PACK)
 
         def z_columns(acc, t, c0, c1):
             nc.tensor.matmul_mx(
@@ -115,7 +123,7 @@ def tile_list_three_point_blend_pl_kernel(
         nc.scalar.copy(out=z[0][:, 0 : T // 2], in_=acc[:, 0 : T // 2])
         acc = banks[1]
         z_columns(acc, 0, T // 2, T)
-        nc.vector.tensor_copy(out=z[0][:, T // 2 : T], in_=acc[:, 0 : T // 2])
+        nc.scalar.copy(out=z[0][:, T // 2 : T], in_=acc[:, 0 : T // 2])
         for t in range(1, PACK):
             acc = banks[(2, 3, 7)[t - 1]]
             z_columns(acc, t, 0, T)

from contextlib import ExitStack

import concourse.mybir as mybir
from concourse.masks import make_identity

K, T, L, J, N = 512, 512, 512, 512, 512
FLOPS = 2 * K * N * T + 2 * L * N * J

F32 = mybir.dt.float32
BF16 = mybir.dt.bfloat16
I32 = mybir.dt.int32
U32 = mybir.dt.uint32
U16 = mybir.dt.uint16
U8 = mybir.dt.uint8
FP8X4 = mybir.dt.float8_e4m3fn_x4
FP4X4 = mybir.dt.float4_e2m1fn_x4
MULT = mybir.AluOpType.mult
ADD = mybir.AluOpType.add

P = 128
PACK = 4
BLOCK = 128
BLOCKS = J // BLOCK
HALF = J // 2
LIST_COLS = 16
RING = 8


def load_scale_rows(queue, plane, rows):
    for q in range(4):
        queue.dma_start(out=plane[32 * q : 32 * q + 4, :].bitcast(I32), in_=rows[0, 4 * q : 4 * q + 4, :].bitcast(I32))


def tile_list_three_point_blend_pl_kernel(
    tc, xt_words, xt_scales, w, sk_words, sk_scales, ws_words, ws_scales, sa, sb, sd, offs, offs2, offs3, out_0, out_1, out_2
):
    nc = tc.nc
    with ExitStack() as ctx:
        sbuf = ctx.enter_context(tc.tile_pool(name="sbuf", bufs=1))
        psum = ctx.enter_context(tc.psum_pool(name="psum", bufs=1))

        banks = [psum.tile([P, 512], F32, name="bank%d" % b) for b in range(8)]
        ring = sbuf.tile([P, RING * HALF], F32)

        lists = [sbuf.tile([P, J // LIST_COLS], U16, name="list%d" % i) for i in range(3)]
        xt_plane = sbuf.tile([P, T], U8, align_bytes=64)
        sk_plane = sbuf.tile([P, J], U8, align_bytes=64)
        ws_plane = sbuf.tile([P, N], U8, align_bytes=64)
        for plane in (xt_plane, sk_plane, ws_plane):
            nc.vector.memset(plane[:].bitcast(U32), 0)
        identity = sbuf.tile([P, P], F32)
        make_identity(nc, identity[:])
        load_scale_rows(nc.gpsimd, ws_plane, ws_scales)

        w_rows = w.rearrange("(p r) n -> p r n", r=PACK)
        w_raw = [sbuf.tile([P, 2, N], F32, name="w_raw%d" % h) for h in range(2)]
        share_cols = [sbuf.tile([P, PACK], F32, name="share_col%d" % i) for i in range(3)]
        share_rows = [share.rearrange("o (q m) -> (o q) m", m=PACK) for share in (sa, sb, sd)]
        nc.sync.dma_start(out=share_cols[0][:], in_=share_rows[0])
        nc.sync.dma_start(out=w_raw[0][:], in_=w_rows[:, 0:2, :])
        nc.sync.dma_start(out=share_cols[1][:], in_=share_rows[1])
        nc.sync.dma_start(out=share_cols[2][:], in_=share_rows[2])
        nc.sync.dma_start(out=w_raw[1][:], in_=w_rows[:, 2:4, :])
        xt_codes = sbuf.tile([P, T], I32, align_bytes=64)
        nc.sync.dma_start(out=xt_codes[:], in_=xt_words[0].rearrange("p c r -> p (c r)").bitcast(I32))
        load_scale_rows(nc.sync, xt_plane, xt_scales)
        for tile, src in zip(lists, (offs, offs2, offs3)):
            nc.sync.dma_start(tile[:], src)
        ws_codes = sbuf.tile([P, N], I32, align_bytes=64)
        nc.sync.dma_start(out=ws_codes[:], in_=ws_words[0].rearrange("p c r -> p (c r)").bitcast(I32))
        sk_codes = sbuf.tile([P, 2 * J], U8, align_bytes=64)
        nc.sync.dma_start(out=sk_codes[:].bitcast(I32), in_=sk_words[0].bitcast(I32))
        load_scale_rows(nc.sync, sk_plane, sk_scales)

        shares = []
        for i in range(3):
            spread = banks[4 + i]
            for m in range(PACK):
                nc.tensor.transpose(spread[:, m * P : (m + 1) * P], share_cols[i][:, m : m + 1].to_broadcast([P, P]), identity[:])
            share = sbuf.tile([P, J], F32, name="share%d" % i)
            nc.scalar.copy(out=share[:].rearrange("p (q m) -> p q m", m=PACK), in_=spread[:].rearrange("p (m q) -> p q m", m=PACK))
            shares.append(share)

        w_bf = sbuf.tile([P, PACK, P, PACK], BF16, align_bytes=64)
        w_codes = sbuf.tile([P, N], U32, align_bytes=64)
        w_plane = sbuf.tile([P, N], U8, align_bytes=64)

        def round_w(h, t0, t1):
            nc.vector.tensor_copy(
                out=w_bf[:, t0:t1, :, 2 * h : 2 * h + 2].rearrange("p t m r -> p m t r"),
                in_=w_raw[h][:].rearrange("p r (m t) -> p m t r", t=PACK)[:, :, t0:t1, :],
            )

        def quantize_w(t0, t1):
            nc.vector.quantize_mx(
                out=w_codes[:, t0 * P : t1 * P].bitcast(FP8X4),
                scales=w_plane[:, t0 * P : t1 * P],
                in_=w_bf[:, t0:t1].rearrange("p t m r -> p (t m r)"),
            )

        round_w(0, 0, PACK)
        round_w(1, 0, 1)
        round_w(1, 1, 2)
        quantize_w(0, 1)
        round_w(1, 2, PACK)
        quantize_w(1, 2)
        quantize_w(2, PACK)

        def z_columns(acc, t, c0, c1):
            nc.tensor.matmul_mx(
                out=acc[:, 0 : c1 - c0],
                lhsT=w_codes[:, t * P : (t + 1) * P].bitcast(FP8X4),
                lhsT_scale=w_plane[:, t * P : (t + 1) * P],
                rhs=xt_codes[:, c0:c1].bitcast(FP8X4),
                rhs_scale=xt_plane[:, c0:c1],
                start=True,
                stop=True,
            )

        z = [sbuf.tile([P, T], F32, name="z%d" % t) for t in range(PACK)]
        acc = banks[0]
        z_columns(acc, 0, 0, T // 2)
        nc.scalar.copy(out=z[0][:, 0 : T // 2], in_=acc[:, 0 : T // 2])
        acc = banks[1]
        z_columns(acc, 0, T // 2, T)
        nc.scalar.copy(out=z[0][:, T // 2 : T], in_=acc[:, 0 : T // 2])
        for t in range(1, PACK):
            acc = banks[(2, 3, 7)[t - 1]]
            z_columns(acc, t, 0, T)
            nc.scalar.copy(out=z[t][:], in_=acc[:])

        skip = []
        for b in range(BLOCKS):
            acc = banks[(4, 5, 6, 0)[b]]
            nc.tensor.matmul_mx(
                out=acc[:],
                lhsT=sk_codes[:, 2 * b * BLOCK : 2 * (b + 1) * BLOCK].bitcast(FP4X4),
                lhsT_scale=sk_plane[:, b * BLOCK : (b + 1) * BLOCK],
                rhs=ws_codes[:].bitcast(FP8X4),
                rhs_scale=ws_plane[:],
                start=True,
                stop=True,
            )
            s_b = sbuf.tile([P, PACK, P], F32, name="skip%d" % b)
            nc.scalar.copy(out=s_b[:], in_=acc[:].rearrange("j (p t) -> j t p", t=PACK))
            skip.append(s_b)

        y_codes = sbuf.tile([P, J], U32, align_bytes=64)
        y_plane = sbuf.tile([P, J], U8, align_bytes=64)
        out_rows = out_0.rearrange("(p t) j -> p t j", t=PACK)
        out_words = out_1[0].rearrange("p c r -> p (c r)").bitcast(I32)

        def gather(out, i, t, j0, j1):
            offsets = lists[i][:, j0 // LIST_COLS : j1 // LIST_COLS]
            nc.vector.tensor_tensor(out, z[t][:].indirect(offsets), shares[i][:, j0:j1], MULT)

        def turn(out, src, start, stop):
            nc.tensor.matmul(out, lhsT=src, rhs=identity[:], is_transpose=True, start=start, stop=stop)

        def summed_on_tensor(half, terms, first, turned_banks, sum_banks):
            blocks = (2 * half, 2 * half + 1)
            turned = [banks[turned_banks[u]] for u in range(2)]
            for t in range(PACK):
                for i in range(terms):
                    slot = (first + t * terms + i) % RING
                    picked = ring[:, slot * HALF : (slot + 1) * HALF]
                    gather(picked, i, t, half * HALF, (half + 1) * HALF)
                    for u in range(2):
                        turn(
                            turned[u][:, t * P : (t + 1) * P],
                            picked[:, u * BLOCK : (u + 1) * BLOCK],
                            t == 0 and i == 0,
                            t == PACK - 1 and i == terms - 1,
                        )
            sums = []
            for u in range(2):
                total = banks[sum_banks[u]]
                for t in range(PACK):
                    turn(total[:, t * BLOCK : (t + 1) * BLOCK], skip[blocks[u]][:, t, :], t == 0, False)
                sums.append(total)
            for u in range(2):
                blend = sbuf.tile([P, PACK * P], F32, name="blend%d" % blocks[u])
                nc.scalar.copy(out=blend[:], in_=turned[u][:])
                for t in range(PACK):
                    turn(sums[u][:, t * BLOCK : (t + 1) * BLOCK], blend[:, t * P : (t + 1) * P], False, t == PACK - 1)
            return sums

        def woven(rows):
            return rows.rearrange("p t (c i) -> p c t i", i=4)

        def quantize(y_bf, j0, j1):
            nc.vector.quantize_mx(
                out=y_codes[:, j0:j1].bitcast(FP8X4), scales=y_plane[:, j0:j1], in_=y_bf[:].rearrange("p j t -> p (j t)")
            )

        sums = summed_on_tensor(0, 3, 0, (4, 5), (1, 2))
        low_bf = sbuf.tile([P, HALF, PACK], BF16, align_bytes=64)
        for b in range(2):
            y_b = sbuf.tile([P, PACK, BLOCK], F32, name="y%d" % b)
            total = sums[b][:].rearrange("p (t j) -> p t j", t=PACK)
            nc.scalar.copy(out=y_b[:], in_=total)
            nc.sync.dma_start(out=out_rows[:, :, b * BLOCK : (b + 1) * BLOCK], in_=y_b[:])
            nc.scalar.copy(out=low_bf[:, b * BLOCK : (b + 1) * BLOCK, :], in_=total.rearrange("p t j -> p j t"))

        sums = summed_on_tensor(1, 2, 12, (4, 5), (3, 7))
        quantize(low_bf, 0, HALF)
        nc.sync.dma_start(out=out_words[:, 0:HALF], in_=y_codes[:, 0:HALF].bitcast(I32))

        high_bf = sbuf.tile([P, HALF, PACK], BF16, align_bytes=64)
        third = ring[:, 4 * HALF : 8 * HALF].rearrange("p (t j) -> p t j", t=PACK)
        for t in range(PACK):
            gather(third[:, t, :], 2, t, HALF, J)
        for b in range(2, BLOCKS):
            last = third[:, :, (b - 2) * BLOCK : (b - 1) * BLOCK]
            total = sums[b - 2][:].rearrange("p (t j) -> p t j", t=PACK)
            y_b = sbuf.tile([P, PACK, BLOCK], F32, name="y%d" % b)
            y_bf = high_bf[:, (b - 2) * BLOCK : (b - 1) * BLOCK, :].rearrange("p (c i) t -> p c t i", i=4)
            if b < BLOCKS - 1:
                nc.vector.tensor_tensor(y_b[:], total, last, ADD)
                nc.scalar.copy(out=y_bf, in_=woven(y_b[:]))
            else:
                nc.vector.tensor_tensor(y_bf, woven(total), woven(last), ADD)
                nc.vector.tensor_tensor(y_b[:], total, last, ADD)
            nc.sync.dma_start(out=out_rows[:, :, b * BLOCK : (b + 1) * BLOCK], in_=y_b[:])
        quantize(high_bf, HALF, J)
        nc.scalar.dma_start(out=out_words[:, HALF:J], in_=y_codes[:, HALF:J].bitcast(I32))
        for q in range(4):
            queue = nc.sync if q % 2 == 0 else nc.scalar
            queue.dma_start(out=out_2[0, 4 * q : 4 * q + 4, :].bitcast(I32), in_=y_plane[32 * q : 32 * q + 4, :].bitcast(I32))
